import numpy as np
import ml_dtypes

BF16 = ml_dtypes.bfloat16


def bf(x):
    return np.asarray(x, np.float32).astype(BF16)


def f32(x):
    return np.asarray(x, np.float32)


def f64(x):
    return np.asarray(x).astype(np.float64)


def striped(idx):
    return np.tile(idx.reshape(-1, 16).T, (8, 1))


S, K, M, N = 4096, 256, 256, 512


def gelu_tanh(v):
    return 0.5 * v * (1.0 + np.tanh(np.sqrt(2.0 / np.pi) * (v + 0.044715 * v**3)))


def setup_inputs():
    return {"table": bf(np.random.standard_normal((S, K))), "w": bf(np.random.standard_normal((K, M)) / np.sqrt(K)), "b": f32(0.5 * np.random.standard_normal((M, 1))), "offs": striped(np.random.permutation(np.tile(np.arange(S), 2))[:N])}


def reference(table, w, b, offs):
    idx = offs[:16].T.reshape(-1)
    x = f64(table)[idx].T
    y = f64(w).T @ x
    return gelu_tanh(y + f64(b))

@@ -1,0 +1,70 @@
+import concourse.mybir as mybir
+from concourse.masks import make_identity
+
+BF16, F32, U16 = mybir.dt.bfloat16, mybir.dt.float32, mybir.dt.uint16
+GELU = mybir.ActivationFunctionType.Gelu_apprx_tanh
+
+P = 128
+S, K, M, N = 4096, 256, 256, 512
+K_BLOCKS = K // P
+M_BLOCKS = M // P
+BANK_WORDS = 1024
+CHUNKS = S // BANK_WORDS
+BLOCKS = BANK_WORDS // P
+
+FLOPS = 2 * K * M * N
+
+
+def tile_gather_matmul_kernel(tc, table, w, b, offs, out):
+    nc = tc.nc
+    with (
+        tc.tile_pool(name="held", bufs=1) as held,
+        tc.tile_pool(name="loaded", bufs=CHUNKS) as loaded,
+        tc.psum_pool(name="flip", bufs=4) as flip,
+        tc.psum_pool(name="sums", bufs=1) as sums,
+    ):
+        offsets = held.tile([P, N // 16], U16, name="offsets")
+        nc.sync.dma_start(offsets[:], offs)
+
+        table_chunks = table.rearrange("(c i p) k -> c p i k", i=BLOCKS, p=P)
+        words = []
+        for c in range(CHUNKS):
+            chunk = loaded.tile([P, BLOCKS, K], BF16, name="chunk")
+            nc.sync.dma_start(chunk[:], table_chunks[c])
+            words.append(chunk)
+
+        weights = held.tile([P, K_BLOCKS, M], BF16, name="weights")
+        nc.scalar.dma_start(weights[:], w.rearrange("(a p) m -> p a m", p=P))
+        bias = held.tile([P, M_BLOCKS], F32, name="bias")
+        nc.scalar.dma_start(bias[:], b.rearrange("(a p) o -> p (a o)", p=P))
+
+        identity = held.tile([P, P], BF16, name="identity")
+        make_identity(nc, identity[:])
+
+        features = [held.tile([P, S], BF16, name="features%d" % a) for a in range(K_BLOCKS)]
+        for c in range(CHUNKS):
+            for a in range(K_BLOCKS):
+                flipped = flip.tile([P, BANK_WORDS], BF16, name="flipped")
+                for i in range(BLOCKS):
+                    nc.tensor.transpose(
+                        flipped[:, i * P : (i + 1) * P], words[c][:, i, a * P : (a + 1) * P], identity[:]
+                    )
+                window_part = features[a][:, c * BANK_WORDS : (c + 1) * BANK_WORDS]
+                if a == 0:
+                    nc.vector.tensor_copy(window_part, flipped[:])
+                else:
+                    nc.scalar.copy(window_part, flipped[:])
+
+        for m in range(M_BLOCKS):
+            y = sums.tile([P, N], F32, name="y%d" % m)
+            for a in range(K_BLOCKS):
+                nc.tensor.matmul(
+                    y[:],
+                    weights[:, a, m * P : (m + 1) * P],
+                    features[a][:].indirect(offsets[:]),
+                    start=(a == 0),
+                    stop=(a == K_BLOCKS - 1),
+                )
+            result = held.tile([P, N], F32, name="result%d" % m)
+            nc.scalar.activation(result[:], y[:], GELU, bias=bias[:, m : m + 1])
+            nc.sync.dma_start(out[m * P : (m + 1) * P, :], result[:])

@@ -8,9 +8,9 @@ P = 128
 S, K, M, N = 4096, 256, 256, 512
 K_BLOCKS = K // P
 M_BLOCKS = M // P
-BANK_WORDS = 1024
-CHUNKS = S // BANK_WORDS
-BLOCKS = BANK_WORDS // P
+CHUNK_WORDS = 512
+CHUNKS = S // CHUNK_WORDS
+BLOCKS = CHUNK_WORDS // P
 
 FLOPS = 2 * K * M * N
 
@@ -20,7 +20,7 @@ def tile_gather_matmul_kernel(tc, table, w, b, offs, out):
     with (
         tc.tile_pool(name="held", bufs=1) as held,
         tc.tile_pool(name="loaded", bufs=CHUNKS) as loaded,
-        tc.psum_pool(name="flip", bufs=4) as flip,
+        tc.psum_pool(name="flip", bufs=6) as flip,
         tc.psum_pool(name="sums", bufs=1) as sums,
     ):
         offsets = held.tile([P, N // 16], U16, name="offsets")
@@ -38,33 +38,39 @@ def tile_gather_matmul_kernel(tc, table, w, b, offs, out):
         bias = held.tile([P, M_BLOCKS], F32, name="bias")
         nc.scalar.dma_start(bias[:], b.rearrange("(a p) o -> p (a o)", p=P))
 
+        zeros = held.tile([P, 1], F32, name="zeros")
+        nc.vector.memset(zeros[:], 0.0)
+        unused = held.tile([P, 1], F32, name="unused")
+        nc.scalar.activation(unused[:], zeros[:], GELU)
+
         identity = held.tile([P, P], BF16, name="identity")
         make_identity(nc, identity[:])
 
         features = [held.tile([P, S], BF16, name="features%d" % a) for a in range(K_BLOCKS)]
         for c in range(CHUNKS):
             for a in range(K_BLOCKS):
-                flipped = flip.tile([P, BANK_WORDS], BF16, name="flipped")
+                flipped = flip.tile([P, CHUNK_WORDS], BF16, name="flipped")
                 for i in range(BLOCKS):
                     nc.tensor.transpose(
                         flipped[:, i * P : (i + 1) * P], words[c][:, i, a * P : (a + 1) * P], identity[:]
                     )
-                window_part = features[a][:, c * BANK_WORDS : (c + 1) * BANK_WORDS]
+                window_part = features[a][:, c * CHUNK_WORDS : (c + 1) * CHUNK_WORDS]
                 if a == 0:
                     nc.vector.tensor_copy(window_part, flipped[:])
                 else:
                     nc.scalar.copy(window_part, flipped[:])
 
-        for m in range(M_BLOCKS):
-            y = sums.tile([P, N], F32, name="y%d" % m)
-            for a in range(K_BLOCKS):
+        y = [sums.tile([P, N], F32, name="y%d" % m) for m in range(M_BLOCKS)]
+        for a in range(K_BLOCKS):
+            for m in range(M_BLOCKS):
                 nc.tensor.matmul(
-                    y[:],
+                    y[m][:],
                     weights[:, a, m * P : (m + 1) * P],
                     features[a][:].indirect(offsets[:]),
                     start=(a == 0),
                     stop=(a == K_BLOCKS - 1),
                 )
+        for m in range(M_BLOCKS):
             result = held.tile([P, N], F32, name="result%d" % m)
-            nc.scalar.activation(result[:], y[:], GELU, bias=bias[:, m : m + 1])
+            nc.scalar.activation(result[:], y[m][:], GELU, bias=bias[:, m : m + 1])
             nc.sync.dma_start(out[m * P : (m + 1) * P, :], result[:])

@@ -11,6 +11,7 @@ M_BLOCKS = M // P
 CHUNK_WORDS = 512
 CHUNKS = S // CHUNK_WORDS
 BLOCKS = CHUNK_WORDS // P
+WARM_MATMULS = 8
 
 FLOPS = 2 * K * M * N
 
@@ -20,7 +21,7 @@ def tile_gather_matmul_kernel(tc, table, w, b, offs, out):
     with (
         tc.tile_pool(name="held", bufs=1) as held,
         tc.tile_pool(name="loaded", bufs=CHUNKS) as loaded,
-        tc.psum_pool(name="flip", bufs=6) as flip,
+        tc.psum_pool(name="flip", bufs=5) as flip,
         tc.psum_pool(name="sums", bufs=1) as sums,
     ):
         offsets = held.tile([P, N // 16], U16, name="offsets")
@@ -42,6 +43,12 @@ def tile_gather_matmul_kernel(tc, table, w, b, offs, out):
         nc.vector.memset(zeros[:], 0.0)
         unused = held.tile([P, 1], F32, name="unused")
         nc.scalar.activation(unused[:], zeros[:], GELU)
+
+        warm_in = held.tile([P, N], BF16, name="warm_in")
+        nc.vector.memset(warm_in[:], 0.0)
+        warm_out = sums.tile([P, N], F32, name="warm_out")
+        for repeat in range(WARM_MATMULS):
+            nc.tensor.matmul(warm_out[:], warm_in[:, 0:P], warm_in[:], start=True, stop=True)
 
         identity = held.tile([P, P], BF16, name="identity")
         make_identity(nc, identity[:])

@@ -6,12 +6,11 @@ GELU = mybir.ActivationFunctionType.Gelu_apprx_tanh
 
 P = 128
 S, K, M, N = 4096, 256, 256, 512
-K_BLOCKS = K // P
 M_BLOCKS = M // P
-CHUNK_WORDS = 512
+PAIR = 2
+ROW_WORDS = 4
+CHUNK_WORDS = P * ROW_WORDS
 CHUNKS = S // CHUNK_WORDS
-BLOCKS = CHUNK_WORDS // P
-WARM_MATMULS = 8
 
 FLOPS = 2 * K * M * N
 
@@ -21,21 +20,21 @@ def tile_gather_matmul_kernel(tc, table, w, b, offs, out):
     with (
         tc.tile_pool(name="held", bufs=1) as held,
         tc.tile_pool(name="loaded", bufs=CHUNKS) as loaded,
-        tc.psum_pool(name="flip", bufs=5) as flip,
+        tc.psum_pool(name="flip", bufs=6) as flip,
         tc.psum_pool(name="sums", bufs=1) as sums,
     ):
         offsets = held.tile([P, N // 16], U16, name="offsets")
         nc.sync.dma_start(offsets[:], offs)
 
-        table_chunks = table.rearrange("(c i p) k -> c p i k", i=BLOCKS, p=P)
+        table_chunks = table.rearrange("(c p r) k -> c p r k", p=P, r=ROW_WORDS)
         words = []
         for c in range(CHUNKS):
-            chunk = loaded.tile([P, BLOCKS, K], BF16, name="chunk")
+            chunk = loaded.tile([P, ROW_WORDS, K], BF16, name="chunk")
             nc.sync.dma_start(chunk[:], table_chunks[c])
             words.append(chunk)
 
-        weights = held.tile([P, K_BLOCKS, M], BF16, name="weights")
-        nc.scalar.dma_start(weights[:], w.rearrange("(a p) m -> p a m", p=P))
+        weights = held.tile([P, PAIR, M], BF16, name="weights")
+        nc.scalar.dma_start(weights[:], w.rearrange("(q e) m -> q e m", e=PAIR))
         bias = held.tile([P, M_BLOCKS], F32, name="bias")
         nc.scalar.dma_start(bias[:], b.rearrange("(a p) o -> p (a o)", p=P))
 
@@ -44,38 +43,34 @@ def tile_gather_matmul_kernel(tc, table, w, b, offs, out):
         unused = held.tile([P, 1], F32, name="unused")
         nc.scalar.activation(unused[:], zeros[:], GELU)
 
-        warm_in = held.tile([P, N], BF16, name="warm_in")
-        nc.vector.memset(warm_in[:], 0.0)
-        warm_out = sums.tile([P, N], F32, name="warm_out")
-        for repeat in range(WARM_MATMULS):
-            nc.tensor.matmul(warm_out[:], warm_in[:, 0:P], warm_in[:], start=True, stop=True)
-
-        identity = held.tile([P, P], BF16, name="identity")
+        identity = held.tile([P, P], F32, name="identity")
         make_identity(nc, identity[:])
 
-        features = [held.tile([P, S], BF16, name="features%d" % a) for a in range(K_BLOCKS)]
+        features = [held.tile([P, S], BF16, name="features%d" % e) for e in range(PAIR)]
         for c in range(CHUNKS):
-            for a in range(K_BLOCKS):
-                flipped = flip.tile([P, CHUNK_WORDS], BF16, name="flipped")
-                for i in range(BLOCKS):
-                    nc.tensor.transpose(
-                        flipped[:, i * P : (i + 1) * P], words[c][:, i, a * P : (a + 1) * P], identity[:]
-                    )
-                window_part = features[a][:, c * CHUNK_WORDS : (c + 1) * CHUNK_WORDS]
-                if a == 0:
-                    nc.vector.tensor_copy(window_part, flipped[:])
+            units = words[c][:].bitcast(F32)
+            flipped = flip.tile([P, ROW_WORDS, P], F32, name="flipped")
+            for r in range(ROW_WORDS):
+                nc.tensor.transpose(flipped[:, r, :], units[:, r, :], identity[:])
+            halves = flipped[:].bitcast(BF16).rearrange("q r (p e) -> q e p r", e=PAIR)
+            for e in range(PAIR):
+                window_part = features[e][:, c * CHUNK_WORDS : (c + 1) * CHUNK_WORDS].rearrange(
+                    "q (p r) -> q p r", r=ROW_WORDS
+                )
+                if e == 0:
+                    nc.vector.tensor_copy(window_part, halves[:, e])
                 else:
-                    nc.scalar.copy(window_part, flipped[:])
+                    nc.scalar.copy(window_part, halves[:, e])
 
         y = [sums.tile([P, N], F32, name="y%d" % m) for m in range(M_BLOCKS)]
-        for a in range(K_BLOCKS):
+        for e in range(PAIR):
             for m in range(M_BLOCKS):
                 nc.tensor.matmul(
                     y[m][:],
-                    weights[:, a, m * P : (m + 1) * P],
-                    features[a][:].indirect(offsets[:]),
-                    start=(a == 0),
-                    stop=(a == K_BLOCKS - 1),
+                    weights[:, e, m * P : (m + 1) * P],
+                    features[e][:].indirect(offsets[:]),
+                    start=(e == 0),
+                    stop=(e == PAIR - 1),
                 )
         for m in range(M_BLOCKS):
             result = held.tile([P, N], F32, name="result%d" % m)

@@ -8,9 +8,10 @@ P = 128
 S, K, M, N = 4096, 256, 256, 512
 M_BLOCKS = M // P
 PAIR = 2
-ROW_WORDS = 4
-CHUNK_WORDS = P * ROW_WORDS
-CHUNKS = S // CHUNK_WORDS
+ROW_WORDS = [2, 2, 4, 4, 4, 4, 4, 4, 2, 2]
+CHUNKS = len(ROW_WORDS)
+FIRST_WORD = [P * sum(ROW_WORDS[:c]) for c in range(CHUNKS + 1)]
+assert FIRST_WORD[CHUNKS] == S
 
 FLOPS = 2 * K * M * N
 
@@ -26,17 +27,18 @@ def tile_gather_matmul_kernel(tc, table, w, b, offs, out):
         offsets = held.tile([P, N // 16], U16, name="offsets")
         nc.sync.dma_start(offsets[:], offs)
 
-        table_chunks = table.rearrange("(c p r) k -> c p r k", p=P, r=ROW_WORDS)
         words = []
         for c in range(CHUNKS):
-            chunk = loaded.tile([P, ROW_WORDS, K], BF16, name="chunk")
-            nc.sync.dma_start(chunk[:], table_chunks[c])
+            chunk = loaded.tile([P, ROW_WORDS[c], K], BF16, name="chunk")
+            nc.sync.dma_start(
+                chunk[:], table[FIRST_WORD[c] : FIRST_WORD[c + 1], :].rearrange("(p r) k -> p r k", r=ROW_WORDS[c])
+            )
             words.append(chunk)
 
         weights = held.tile([P, PAIR, M], BF16, name="weights")
-        nc.scalar.dma_start(weights[:], w.rearrange("(q e) m -> q e m", e=PAIR))
+        nc.sync.dma_start(weights[:], w.rearrange("(q e) m -> q e m", e=PAIR))
         bias = held.tile([P, M_BLOCKS], F32, name="bias")
-        nc.scalar.dma_start(bias[:], b.rearrange("(a p) o -> p (a o)", p=P))
+        nc.sync.dma_start(bias[:], b.rearrange("(a p) o -> p (a o)", p=P))
 
         zeros = held.tile([P, 1], F32, name="zeros")
         nc.vector.memset(zeros[:], 0.0)
@@ -49,13 +51,13 @@ def tile_gather_matmul_kernel(tc, table, w, b, offs, out):
         features = [held.tile([P, S], BF16, name="features%d" % e) for e in range(PAIR)]
         for c in range(CHUNKS):
             units = words[c][:].bitcast(F32)
-            flipped = flip.tile([P, ROW_WORDS, P], F32, name="flipped")
-            for r in range(ROW_WORDS):
+            flipped = flip.tile([P, ROW_WORDS[c], P], F32, name="flipped")
+            for r in range(ROW_WORDS[c]):
                 nc.tensor.transpose(flipped[:, r, :], units[:, r, :], identity[:])
             halves = flipped[:].bitcast(BF16).rearrange("q r (p e) -> q e p r", e=PAIR)
             for e in range(PAIR):
-                window_part = features[e][:, c * CHUNK_WORDS : (c + 1) * CHUNK_WORDS].rearrange(
-                    "q (p r) -> q p r", r=ROW_WORDS
+                window_part = features[e][:, FIRST_WORD[c] : FIRST_WORD[c + 1]].rearrange(
+                    "q (p r) -> q p r", r=ROW_WORDS[c]
                 )
                 if e == 0:
                     nc.vector.tensor_copy(window_part, halves[:, e])

@@ -13,6 +13,9 @@ CHUNKS = len(ROW_WORDS)
 FIRST_WORD = [P * sum(ROW_WORDS[:c]) for c in range(CHUNKS + 1)]
 assert FIRST_WORD[CHUNKS] == S
 
+HEAD_WARMERS = 4
+WARMED_CHUNKS = range(3, 8)
+
 FLOPS = 2 * K * M * N
 
 
@@ -48,12 +51,26 @@ def tile_gather_matmul_kernel(tc, table, w, b, offs, out):
         identity = held.tile([P, P], F32, name="identity")
         make_identity(nc, identity[:])
 
+        y = [sums.tile([P, N], F32, name="y%d" % m) for m in range(M_BLOCKS)]
+        nothing = held.tile([P, N], BF16, name="nothing")
+        nc.vector.memset(nothing[:], 0.0)
+        for i in range(HEAD_WARMERS):
+            nc.tensor.matmul(y[0][:], nothing[:, 0:P], nothing[:], start=True, stop=True)
+
         features = [held.tile([P, S], BF16, name="features%d" % e) for e in range(PAIR)]
         for c in range(CHUNKS):
             units = words[c][:].bitcast(F32)
             flipped = flip.tile([P, ROW_WORDS[c], P], F32, name="flipped")
             for r in range(ROW_WORDS[c]):
                 nc.tensor.transpose(flipped[:, r, :], units[:, r, :], identity[:])
+            if c in WARMED_CHUNKS:
+                nc.tensor.matmul(
+                    y[0][:],
+                    nothing[:, 0:P],
+                    features[0][:, FIRST_WORD[c - 1] - N : FIRST_WORD[c - 1]],
+                    start=True,
+                    stop=True,
+                )
             halves = flipped[:].bitcast(BF16).rearrange("q r (p e) -> q e p r", e=PAIR)
             for e in range(PAIR):
                 window_part = features[e][:, FIRST_WORD[c] : FIRST_WORD[c + 1]].rearrange(
@@ -64,7 +81,6 @@ def tile_gather_matmul_kernel(tc, table, w, b, offs, out):
                 else:
                     nc.scalar.copy(window_part, halves[:, e])
 
-        y = [sums.tile([P, N], F32, name="y%d" % m) for m in range(M_BLOCKS)]
         for e in range(PAIR):
             for m in range(M_BLOCKS):
                 nc.tensor.matmul(

@@ -8,12 +8,15 @@ P = 128
 S, K, M, N = 4096, 256, 256, 512
 M_BLOCKS = M // P
 PAIR = 2
-ROW_WORDS = [2, 2, 4, 4, 4, 4, 4, 4, 2, 2]
+ROW_WORDS = [2, 2, 4, 4, 4, 4, 4, 4]
 CHUNKS = len(ROW_WORDS)
 FIRST_WORD = [P * sum(ROW_WORDS[:c]) for c in range(CHUNKS + 1)]
-assert FIRST_WORD[CHUNKS] == S
+END_BLOCKS = [2, 2]
+END_CHUNKS = len(END_BLOCKS)
+END_FIRST_WORD = [FIRST_WORD[CHUNKS] + P * sum(END_BLOCKS[:t]) for t in range(END_CHUNKS + 1)]
+assert END_FIRST_WORD[END_CHUNKS] == S
 
-HEAD_WARMERS = 4
+HEAD_WARMERS = 2
 WARMED_CHUNKS = range(3, 8)
 
 FLOPS = 2 * K * M * N
@@ -24,12 +27,10 @@ def tile_gather_matmul_kernel(tc, table, w, b, offs, out):
     with (
         tc.tile_pool(name="held", bufs=1) as held,
         tc.tile_pool(name="loaded", bufs=CHUNKS) as loaded,
+        tc.tile_pool(name="loaded_end", bufs=END_CHUNKS) as loaded_end,
         tc.psum_pool(name="flip", bufs=6) as flip,
         tc.psum_pool(name="sums", bufs=1) as sums,
     ):
-        offsets = held.tile([P, N // 16], U16, name="offsets")
-        nc.sync.dma_start(offsets[:], offs)
-
         words = []
         for c in range(CHUNKS):
             chunk = loaded.tile([P, ROW_WORDS[c], K], BF16, name="chunk")
@@ -37,7 +38,16 @@ def tile_gather_matmul_kernel(tc, table, w, b, offs, out):
                 chunk[:], table[FIRST_WORD[c] : FIRST_WORD[c + 1], :].rearrange("(p r) k -> p r k", r=ROW_WORDS[c])
             )
             words.append(chunk)
+        end_words = []
+        for t in range(END_CHUNKS):
+            end_chunk = loaded_end.tile([P, END_BLOCKS[t], K], BF16, name="end_chunk")
+            nc.sync.dma_start(
+                end_chunk[:], table[END_FIRST_WORD[t] : END_FIRST_WORD[t + 1], :].rearrange("(s p) k -> p s k", p=P)
+            )
+            end_words.append(end_chunk)
 
+        offsets = held.tile([P, N // 16], U16, name="offsets")
+        nc.sync.dma_start(offsets[:], offs)
         weights = held.tile([P, PAIR, M], BF16, name="weights")
         nc.sync.dma_start(weights[:], w.rearrange("(q e) m -> q e m", e=PAIR))
         bias = held.tile([P, M_BLOCKS], F32, name="bias")
@@ -50,6 +60,8 @@ def tile_gather_matmul_kernel(tc, table, w, b, offs, out):
 
         identity = held.tile([P, P], F32, name="identity")
         make_identity(nc, identity[:])
+        identity_bf16 = held.tile([P, P], BF16, name="identity_bf16")
+        make_identity(nc, identity_bf16[:])
 
         y = [sums.tile([P, N], F32, name="y%d" % m) for m in range(M_BLOCKS)]
         nothing = held.tile([P, N], BF16, name="nothing")
@@ -80,6 +92,18 @@ def tile_gather_matmul_kernel(tc, table, w, b, offs, out):
                     nc.vector.tensor_copy(window_part, halves[:, e])
                 else:
                     nc.scalar.copy(window_part, halves[:, e])
+
+        for t in range(END_CHUNKS):
+            by_parity = end_words[t][:].rearrange("p s (q e) -> p s e q", e=PAIR)
+            for e in range(PAIR):
+                flipped_half = flip.tile([P, END_BLOCKS[t] * P], BF16, name="flipped_half", tag="flipped")
+                for s in range(END_BLOCKS[t]):
+                    nc.tensor.transpose(flipped_half[:, s * P : (s + 1) * P], by_parity[:, s, e, :], identity_bf16[:])
+                window_part = features[e][:, END_FIRST_WORD[t] : END_FIRST_WORD[t + 1]]
+                if e == 0:
+                    nc.vector.tensor_copy(window_part, flipped_half[:])
+                else:
+                    nc.scalar.copy(window_part, flipped_half[:])
 
         for e in range(PAIR):
             for m in range(M_BLOCKS):

@@ -16,7 +16,7 @@ END_CHUNKS = len(END_BLOCKS)
 END_FIRST_WORD = [FIRST_WORD[CHUNKS] + P * sum(END_BLOCKS[:t]) for t in range(END_CHUNKS + 1)]
 assert END_FIRST_WORD[END_CHUNKS] == S
 
-HEAD_WARMERS = 2
+HEAD_WARMERS = 4
 WARMED_CHUNKS = range(3, 8)
 
 FLOPS = 2 * K * M * N

@@ -18,6 +18,7 @@ assert END_FIRST_WORD[END_CHUNKS] == S
 
 HEAD_WARMERS = 4
 WARMED_CHUNKS = range(3, 8)
+WARMER_COLUMNS = 512
 
 FLOPS = 2 * K * M * N
 
@@ -53,6 +54,12 @@ def tile_gather_matmul_kernel(tc, table, w, b, offs, out):
         bias = held.tile([P, M_BLOCKS], F32, name="bias")
         nc.sync.dma_start(bias[:], b.rearrange("(a p) o -> p (a o)", p=P))
 
+        y = [sums.tile([P, N], F32, name="y%d" % m) for m in range(M_BLOCKS)]
+        nothing = held.tile([P, P], BF16, name="nothing")
+        nc.gpsimd.memset(nothing[:], 0.0)
+        for i in range(HEAD_WARMERS):
+            nc.tensor.matmul(y[0][:], nothing[:], nothing[:].unsqueeze(1).to_broadcast([P, N // P, P]), start=True, stop=True)
+
         zeros = held.tile([P, 1], F32, name="zeros")
         nc.vector.memset(zeros[:], 0.0)
         unused = held.tile([P, 1], F32, name="unused")
@@ -63,12 +70,6 @@ def tile_gather_matmul_kernel(tc, table, w, b, offs, out):
         identity_bf16 = held.tile([P, P], BF16, name="identity_bf16")
         make_identity(nc, identity_bf16[:])
 
-        y = [sums.tile([P, N], F32, name="y%d" % m) for m in range(M_BLOCKS)]
-        nothing = held.tile([P, N], BF16, name="nothing")
-        nc.vector.memset(nothing[:], 0.0)
-        for i in range(HEAD_WARMERS):
-            nc.tensor.matmul(y[0][:], nothing[:, 0:P], nothing[:], start=True, stop=True)
-
         features = [held.tile([P, S], BF16, name="features%d" % e) for e in range(PAIR)]
         for c in range(CHUNKS):
             units = words[c][:].bitcast(F32)
@@ -77,9 +78,9 @@ def tile_gather_matmul_kernel(tc, table, w, b, offs, out):
                 nc.tensor.transpose(flipped[:, r, :], units[:, r, :], identity[:])
             if c in WARMED_CHUNKS:
                 nc.tensor.matmul(
-                    y[0][:],
-                    nothing[:, 0:P],
-                    features[0][:, FIRST_WORD[c - 1] - N : FIRST_WORD[c - 1]],
+                    y[0][:, 0:WARMER_COLUMNS],
+                    nothing[:],
+                    features[0][:, FIRST_WORD[c - 1] - WARMER_COLUMNS : FIRST_WORD[c - 1]],
                     start=True,
                     stop=True,
                 )

@@ -20,6 +20,8 @@ HEAD_WARMERS = 4
 WARMED_CHUNKS = range(3, 8)
 WARMER_COLUMNS = 512
 
+DMA_ALIGN = 256
+
 FLOPS = 2 * K * M * N
 
 
@@ -34,14 +36,14 @@ def tile_gather_matmul_kernel(tc, table, w, b, offs, out):
     ):
         words = []
         for c in range(CHUNKS):
-            chunk = loaded.tile([P, ROW_WORDS[c], K], BF16, name="chunk")
+            chunk = loaded.tile([P, ROW_WORDS[c], K], BF16, name="chunk", align_bytes=DMA_ALIGN)
             nc.sync.dma_start(
                 chunk[:], table[FIRST_WORD[c] : FIRST_WORD[c + 1], :].rearrange("(p r) k -> p r k", r=ROW_WORDS[c])
             )
             words.append(chunk)
         end_words = []
         for t in range(END_CHUNKS):
-            end_chunk = loaded_end.tile([P, END_BLOCKS[t], K], BF16, name="end_chunk")
+            end_chunk = loaded_end.tile([P, END_BLOCKS[t], K], BF16, name="end_chunk", align_bytes=DMA_ALIGN)
             nc.sync.dma_start(
                 end_chunk[:], table[END_FIRST_WORD[t] : END_FIRST_WORD[t + 1], :].rearrange("(s p) k -> p s k", p=P)
             )
@@ -49,7 +51,7 @@ def tile_gather_matmul_kernel(tc, table, w, b, offs, out):
 
         offsets = held.tile([P, N // 16], U16, name="offsets")
         nc.sync.dma_start(offsets[:], offs)
-        weights = held.tile([P, PAIR, M], BF16, name="weights")
+        weights = held.tile([P, PAIR, M], BF16, name="weights", align_bytes=DMA_ALIGN)
         nc.sync.dma_start(weights[:], w.rearrange("(q e) m -> q e m", e=PAIR))
         bias = held.tile([P, M_BLOCKS], F32, name="bias")
         nc.sync.dma_start(bias[:], b.rearrange("(a p) o -> p (a o)", p=P))
@@ -116,6 +118,6 @@ def tile_gather_matmul_kernel(tc, table, w, b, offs, out):
                     stop=(e == PAIR - 1),
                 )
         for m in range(M_BLOCKS):
-            result = held.tile([P, N], F32, name="result%d" % m)
+            result = held.tile([P, N], F32, name="result%d" % m, align_bytes=DMA_ALIGN)
             nc.scalar.activation(result[:], y[m][:], GELU, bias=bias[:, m : m + 1])
             nc.sync.dma_start(out[m * P : (m + 1) * P, :], result[:])

@@ -20,7 +20,7 @@ HEAD_WARMERS = 4
 WARMED_CHUNKS = range(3, 8)
 WARMER_COLUMNS = 512
 
-DMA_ALIGN = 256
+DMA_ALIGN = 2048
 
 FLOPS = 2 * K * M * N
 
@@ -72,7 +72,7 @@ def tile_gather_matmul_kernel(tc, table, w, b, offs, out):
         identity_bf16 = held.tile([P, P], BF16, name="identity_bf16")
         make_identity(nc, identity_bf16[:])
 
-        features = [held.tile([P, S], BF16, name="features%d" % e) for e in range(PAIR)]
+        features = [held.tile([P, S], BF16, name="features%d" % e, align_bytes=DMA_ALIGN) for e in range(PAIR)]
         for c in range(CHUNKS):
             units = words[c][:].bitcast(F32)
             flipped = flip.tile([P, ROW_WORDS[c], P], F32, name="flipped")

@@ -52,7 +52,9 @@ def tile_gather_matmul_kernel(tc, table, w, b, offs, out):
         offsets = held.tile([P, N // 16], U16, name="offsets")
         nc.sync.dma_start(offsets[:], offs)
         weights = held.tile([P, PAIR, M], BF16, name="weights", align_bytes=DMA_ALIGN)
-        nc.sync.dma_start(weights[:], w.rearrange("(q e) m -> q e m", e=PAIR))
+        rows_by_parity = w.rearrange("(q e) m -> q e m", e=PAIR)
+        for e in range(PAIR):
+            nc.sync.dma_start(weights[:, e, :], rows_by_parity[:, e, :])
         bias = held.tile([P, M_BLOCKS], F32, name="bias")
         nc.sync.dma_start(bias[:], b.rearrange("(a p) o -> p (a o)", p=P))
 

@@ -11,7 +11,7 @@ PAIR = 2
 ROW_WORDS = [2, 2, 4, 4, 4, 4, 4, 4]
 CHUNKS = len(ROW_WORDS)
 FIRST_WORD = [P * sum(ROW_WORDS[:c]) for c in range(CHUNKS + 1)]
-END_BLOCKS = [2, 2]
+END_BLOCKS = [3, 1]
 END_CHUNKS = len(END_BLOCKS)
 END_FIRST_WORD = [FIRST_WORD[CHUNKS] + P * sum(END_BLOCKS[:t]) for t in range(END_CHUNKS + 1)]
 assert END_FIRST_WORD[END_CHUNKS] == S

@@ -8,16 +8,16 @@ P = 128
 S, K, M, N = 4096, 256, 256, 512
 M_BLOCKS = M // P
 PAIR = 2
-ROW_WORDS = [2, 2, 4, 4, 4, 4, 4, 4]
+ROW_WORDS = [2, 2, 4, 4, 4, 4, 4]
 CHUNKS = len(ROW_WORDS)
 FIRST_WORD = [P * sum(ROW_WORDS[:c]) for c in range(CHUNKS + 1)]
-END_BLOCKS = [3, 1]
+END_BLOCKS = [4, 3, 1]
 END_CHUNKS = len(END_BLOCKS)
 END_FIRST_WORD = [FIRST_WORD[CHUNKS] + P * sum(END_BLOCKS[:t]) for t in range(END_CHUNKS + 1)]
 assert END_FIRST_WORD[END_CHUNKS] == S
 
 HEAD_WARMERS = 4
-WARMED_CHUNKS = range(3, 8)
+WARMED_CHUNKS = range(3, 7)
 WARMER_COLUMNS = 512
 
 DMA_ALIGN = 2048
@@ -98,9 +98,9 @@ def tile_gather_matmul_kernel(tc, table, w, b, offs, out):
                 else:
                     nc.scalar.copy(window_part, halves[:, e])
 
-        for t in range(END_CHUNKS):
-            by_parity = end_words[t][:].rearrange("p s (q e) -> p s e q", e=PAIR)
-            for e in range(PAIR):
+        for e in range(PAIR):
+            for t in range(END_CHUNKS):
+                by_parity = end_words[t][:].rearrange("p s (q e) -> p s e q", e=PAIR)
                 flipped_half = flip.tile([P, END_BLOCKS[t] * P], BF16, name="flipped_half", tag="flipped")
                 for s in range(END_BLOCKS[t]):
                     nc.tensor.transpose(flipped_half[:, s * P : (s + 1) * P], by_parity[:, s, e, :], identity_bf16[:])

@@ -105,10 +105,7 @@ def tile_gather_matmul_kernel(tc, table, w, b, offs, out):
                 for s in range(END_BLOCKS[t]):
                     nc.tensor.transpose(flipped_half[:, s * P : (s + 1) * P], by_parity[:, s, e, :], identity_bf16[:])
                 window_part = features[e][:, END_FIRST_WORD[t] : END_FIRST_WORD[t + 1]]
-                if e == 0:
-                    nc.vector.tensor_copy(window_part, flipped_half[:])
-                else:
-                    nc.scalar.copy(window_part, flipped_half[:])
+                nc.vector.tensor_copy(window_part, flipped_half[:])
 
         for e in range(PAIR):
             for m in range(M_BLOCKS):

@@ -58,7 +58,7 @@ def tile_gather_matmul_kernel(tc, table, w, b, offs, out):
         bias = held.tile([P, M_BLOCKS], F32, name="bias")
         nc.sync.dma_start(bias[:], b.rearrange("(a p) o -> p (a o)", p=P))
 
-        y = [sums.tile([P, N], F32, name="y%d" % m) for m in range(M_BLOCKS)]
+        y = [sums.tile([P, N], F32, name="y0")]
         nothing = held.tile([P, P], BF16, name="nothing")
         nc.gpsimd.memset(nothing[:], 0.0)
         for i in range(HEAD_WARMERS):
@@ -101,14 +101,21 @@ def tile_gather_matmul_kernel(tc, table, w, b, offs, out):
         for e in range(PAIR):
             for t in range(END_CHUNKS):
                 by_parity = end_words[t][:].rearrange("p s (q e) -> p s e q", e=PAIR)
-                flipped_half = flip.tile([P, END_BLOCKS[t] * P], BF16, name="flipped_half", tag="flipped")
+                if e == PAIR - 1 and t == END_CHUNKS - 1:
+                    flipped_half = sums.tile([P, END_BLOCKS[t] * P], BF16, name="flipped_half", tag="y1")
+                else:
+                    flipped_half = flip.tile([P, END_BLOCKS[t] * P], BF16, name="flipped_half", tag="flipped")
                 for s in range(END_BLOCKS[t]):
                     nc.tensor.transpose(flipped_half[:, s * P : (s + 1) * P], by_parity[:, s, e, :], identity_bf16[:])
                 window_part = features[e][:, END_FIRST_WORD[t] : END_FIRST_WORD[t + 1]]
-                nc.vector.tensor_copy(window_part, flipped_half[:])
+                if e == 0 or t % 2 == 1:
+                    nc.vector.tensor_copy(window_part, flipped_half[:])
+                else:
+                    nc.scalar.copy(window_part, flipped_half[:])
 
-        for e in range(PAIR):
-            for m in range(M_BLOCKS):
+        y.append(sums.tile([P, N], F32, name="y1"))
+        for m in range(M_BLOCKS):
+            for e in range(PAIR):
                 nc.tensor.matmul(
                     y[m][:],
                     weights[:, e, m * P : (m + 1) * P],

@@ -17,8 +17,7 @@ END_FIRST_WORD = [FIRST_WORD[CHUNKS] + P * sum(END_BLOCKS[:t]) for t in range(EN
 assert END_FIRST_WORD[END_CHUNKS] == S
 
 HEAD_WARMERS = 4
-WARMED_CHUNKS = range(3, 7)
-WARMER_COLUMNS = 512
+WARMER_WORDS = 2
 
 DMA_ALIGN = 2048
 
@@ -80,14 +79,7 @@ def tile_gather_matmul_kernel(tc, table, w, b, offs, out):
             flipped = flip.tile([P, ROW_WORDS[c], P], F32, name="flipped")
             for r in range(ROW_WORDS[c]):
                 nc.tensor.transpose(flipped[:, r, :], units[:, r, :], identity[:])
-            if c in WARMED_CHUNKS:
-                nc.tensor.matmul(
-                    y[0][:, 0:WARMER_COLUMNS],
-                    nothing[:],
-                    features[0][:, FIRST_WORD[c - 1] - WARMER_COLUMNS : FIRST_WORD[c - 1]],
-                    start=True,
-                    stop=True,
-                )
+            nc.tensor.matmul(y[0][:], identity_bf16[:], words[c][:, 0:WARMER_WORDS, :], start=True, stop=True)
             halves = flipped[:].bitcast(BF16).rearrange("q r (p e) -> q e p r", e=PAIR)
             for e in range(PAIR):
                 window_part = features[e][:, FIRST_WORD[c] : FIRST_WORD[c + 1]].rearrange(

@@ -19,6 +19,8 @@ assert END_FIRST_WORD[END_CHUNKS] == S
 HEAD_WARMERS = 4
 WARMER_WORDS = 2
 
+LAST_PIECES = 2
+
 DMA_ALIGN = 2048
 
 FLOPS = 2 * K * M * N
@@ -51,9 +53,7 @@ def tile_gather_matmul_kernel(tc, table, w, b, offs, out):
         offsets = held.tile([P, N // 16], U16, name="offsets")
         nc.sync.dma_start(offsets[:], offs)
         weights = held.tile([P, PAIR, M], BF16, name="weights", align_bytes=DMA_ALIGN)
-        rows_by_parity = w.rearrange("(q e) m -> q e m", e=PAIR)
-        for e in range(PAIR):
-            nc.sync.dma_start(weights[:, e, :], rows_by_parity[:, e, :])
+        nc.sync.dma_start(weights[:], w.rearrange("(q e) m -> q e m", e=PAIR))
         bias = held.tile([P, M_BLOCKS], F32, name="bias")
         nc.sync.dma_start(bias[:], b.rearrange("(a p) o -> p (a o)", p=P))
 
@@ -117,5 +117,8 @@ def tile_gather_matmul_kernel(tc, table, w, b, offs, out):
                 )
         for m in range(M_BLOCKS):
             result = held.tile([P, N], F32, name="result%d" % m, align_bytes=DMA_ALIGN)
-            nc.scalar.activation(result[:], y[m][:], GELU, bias=bias[:, m : m + 1])
-            nc.sync.dma_start(out[m * P : (m + 1) * P, :], result[:])
+            pieces = LAST_PIECES if m == M_BLOCKS - 1 else 1
+            for i in range(pieces):
+                tokens = slice(i * (N // pieces), (i + 1) * (N // pieces))
+                nc.scalar.activation(result[:, tokens], y[m][:, tokens], GELU, bias=bias[:, m : m + 1])
+                nc.sync.dma_start(out[m * P : (m + 1) * P, tokens], result[:, tokens])

@@ -8,7 +8,7 @@ P = 128
 S, K, M, N = 4096, 256, 256, 512
 M_BLOCKS = M // P
 PAIR = 2
-ROW_WORDS = [2, 2, 4, 4, 4, 4, 4]
+ROW_WORDS = [4, 4, 4, 4, 4, 4]
 CHUNKS = len(ROW_WORDS)
 FIRST_WORD = [P * sum(ROW_WORDS[:c]) for c in range(CHUNKS + 1)]
 END_BLOCKS = [4, 3, 1]
@@ -53,7 +53,9 @@ def tile_gather_matmul_kernel(tc, table, w, b, offs, out):
         offsets = held.tile([P, N // 16], U16, name="offsets")
         nc.sync.dma_start(offsets[:], offs)
         weights = held.tile([P, PAIR, M], BF16, name="weights", align_bytes=DMA_ALIGN)
-        nc.sync.dma_start(weights[:], w.rearrange("(q e) m -> q e m", e=PAIR))
+        rows_by_parity = w.rearrange("(q e) m -> q e m", e=PAIR)
+        for e in range(PAIR):
+            nc.sync.dma_start(weights[:, e, :], rows_by_parity[:, e, :])
         bias = held.tile([P, M_BLOCKS], F32, name="bias")
         nc.sync.dma_start(bias[:], b.rearrange("(a p) o -> p (a o)", p=P))
 

import concourse.mybir as mybir
from concourse.masks import make_identity

BF16, F32, U16 = mybir.dt.bfloat16, mybir.dt.float32, mybir.dt.uint16
GELU = mybir.ActivationFunctionType.Gelu_apprx_tanh

P = 128
S, K, M, N = 4096, 256, 256, 512
M_BLOCKS = M // P
PAIR = 2
ROW_WORDS = [4, 4, 4, 4, 4, 4]
CHUNKS = len(ROW_WORDS)
FIRST_WORD = [P * sum(ROW_WORDS[:c]) for c in range(CHUNKS + 1)]
END_BLOCKS = [4, 3, 1]
END_CHUNKS = len(END_BLOCKS)
END_FIRST_WORD = [FIRST_WORD[CHUNKS] + P * sum(END_BLOCKS[:t]) for t in range(END_CHUNKS + 1)]
assert END_FIRST_WORD[END_CHUNKS] == S

HEAD_WARMERS = 4
WARMER_WORDS = 2

LAST_PIECES = 2

DMA_ALIGN = 2048

FLOPS = 2 * K * M * N


def tile_gather_matmul_kernel(tc, table, w, b, offs, out):
    nc = tc.nc
    with (
        tc.tile_pool(name="held", bufs=1) as held,
        tc.tile_pool(name="loaded", bufs=CHUNKS) as loaded,
        tc.tile_pool(name="loaded_end", bufs=END_CHUNKS) as loaded_end,
        tc.psum_pool(name="flip", bufs=6) as flip,
        tc.psum_pool(name="sums", bufs=1) as sums,
    ):
        words = []
        for c in range(CHUNKS):
            chunk = loaded.tile([P, ROW_WORDS[c], K], BF16, name="chunk", align_bytes=DMA_ALIGN)
            nc.sync.dma_start(
                chunk[:], table[FIRST_WORD[c] : FIRST_WORD[c + 1], :].rearrange("(p r) k -> p r k", r=ROW_WORDS[c])
            )
            words.append(chunk)
        end_words = []
        for t in range(END_CHUNKS):
            end_chunk = loaded_end.tile([P, END_BLOCKS[t], K], BF16, name="end_chunk", align_bytes=DMA_ALIGN)
            nc.sync.dma_start(
                end_chunk[:], table[END_FIRST_WORD[t] : END_FIRST_WORD[t + 1], :].rearrange("(s p) k -> p s k", p=P)
            )
            end_words.append(end_chunk)

        offsets = held.tile([P, N // 16], U16, name="offsets")
        nc.sync.dma_start(offsets[:], offs)
        weights = held.tile([P, PAIR, M], BF16, name="weights", align_bytes=DMA_ALIGN)
        rows_by_parity = w.rearrange("(q e) m -> q e m", e=PAIR)
        for e in range(PAIR):
            nc.sync.dma_start(weights[:, e, :], rows_by_parity[:, e, :])
        bias = held.tile([P, M_BLOCKS], F32, name="bias")
        nc.sync.dma_start(bias[:], b.rearrange("(a p) o -> p (a o)", p=P))

        y = [sums.tile([P, N], F32, name="y0")]
        nothing = held.tile([P, P], BF16, name="nothing")
        nc.gpsimd.memset(nothing[:], 0.0)
        for i in range(HEAD_WARMERS):
            nc.tensor.matmul(y[0][:], nothing[:], nothing[:].unsqueeze(1).to_broadcast([P, N // P, P]), start=True, stop=True)

        zeros = held.tile([P, 1], F32, name="zeros")
        nc.vector.memset(zeros[:], 0.0)
        unused = held.tile([P, 1], F32, name="unused")
        nc.scalar.activation(unused[:], zeros[:], GELU)

        identity = held.tile([P, P], F32, name="identity")
        make_identity(nc, identity[:])
        identity_bf16 = held.tile([P, P], BF16, name="identity_bf16")
        make_identity(nc, identity_bf16[:])

        features = [held.tile([P, S], BF16, name="features%d" % e, align_bytes=DMA_ALIGN) for e in range(PAIR)]
        for c in range(CHUNKS):
            units = words[c][:].bitcast(F32)
            flipped = flip.tile([P, ROW_WORDS[c], P], F32, name="flipped")
            for r in range(ROW_WORDS[c]):
                nc.tensor.transpose(flipped[:, r, :], units[:, r, :], identity[:])
            nc.tensor.matmul(y[0][:], identity_bf16[:], words[c][:, 0:WARMER_WORDS, :], start=True, stop=True)
            halves = flipped[:].bitcast(BF16).rearrange("q r (p e) -> q e p r", e=PAIR)
            for e in range(PAIR):
                window_part = features[e][:, FIRST_WORD[c] : FIRST_WORD[c + 1]].rearrange(
                    "q (p r) -> q p r", r=ROW_WORDS[c]
                )
                if e == 0:
                    nc.vector.tensor_copy(window_part, halves[:, e])
                else:
                    nc.scalar.copy(window_part, halves[:, e])

        for e in range(PAIR):
            for t in range(END_CHUNKS):
                by_parity = end_words[t][:].rearrange("p s (q e) -> p s e q", e=PAIR)
                if e == PAIR - 1 and t == END_CHUNKS - 1:
                    flipped_half = sums.tile([P, END_BLOCKS[t] * P], BF16, name="flipped_half", tag="y1")
                else:
                    flipped_half = flip.tile([P, END_BLOCKS[t] * P], BF16, name="flipped_half", tag="flipped")
                for s in range(END_BLOCKS[t]):
                    nc.tensor.transpose(flipped_half[:, s * P : (s + 1) * P], by_parity[:, s, e, :], identity_bf16[:])
                window_part = features[e][:, END_FIRST_WORD[t] : END_FIRST_WORD[t + 1]]
                if e == 0 or t % 2 == 1:
                    nc.vector.tensor_copy(window_part, flipped_half[:])
                else:
                    nc.scalar.copy(window_part, flipped_half[:])

        y.append(sums.tile([P, N], F32, name="y1"))
        for m in range(M_BLOCKS):
            for e in range(PAIR):
                nc.tensor.matmul(
                    y[m][:],
                    weights[:, e, m * P : (m + 1) * P],
                    features[e][:].indirect(offsets[:]),
                    start=(e == 0),
                    stop=(e == PAIR - 1),
                )
        for m in range(M_BLOCKS):
            result = held.tile([P, N], F32, name="result%d" % m, align_bytes=DMA_ALIGN)
            pieces = LAST_PIECES if m == M_BLOCKS - 1 else 1
            for i in range(pieces):
                tokens = slice(i * (N // pieces), (i + 1) * (N // pieces))
                nc.scalar.activation(result[:, tokens], y[m][:, tokens], GELU, bias=bias[:, m : m + 1])
                nc.sync.dma_start(out[m * P : (m + 1) * P, tokens], result[:, tokens])
